import numpy as np
import ml_dtypes


def mxq(x, axis, fmt="e4m3"):
    dtype, down = {"e4m3": (ml_dtypes.float8_e4m3fn, 7), "e5m2": (ml_dtypes.float8_e5m2, 14)}[fmt]
    v = np.moveaxis(np.asarray(x, np.float32).astype(ml_dtypes.bfloat16).astype(np.float64), axis, -1)
    blocks = v.reshape(v.shape[:-1] + (-1, 32))
    amax = np.abs(blocks).max(-1, keepdims=True)
    byte = np.maximum(np.where(amax > 0, np.frexp(amax)[1] - 1 + 127, 0) - down, 1)
    scale = np.exp2(byte - 127.0)
    codes = (blocks / scale).astype(np.float32).astype(dtype).astype(np.float64)
    return np.moveaxis((codes * scale).reshape(v.shape), -1, axis)


WIDE = False


def mx_kscale(k):
    if not WIDE:
        return np.ones(k)
    levels = np.array([10, -10, 5, -5, 0])
    if k % 512:
        return np.exp2(np.random.permutation(np.resize(levels, k // 32))).repeat(32)
    a = np.empty((k // 512, 16))
    for p in range(k // 512):
        a[p, :8] = np.random.permutation(np.resize(levels, 8))
        for g in range(8):
            far = levels[np.abs(levels - a[p, g]) >= 10]
            a[p, g + 8] = far[np.random.randint(len(far))]
    return np.exp2(a.ravel()).repeat(32)


BF16 = ml_dtypes.bfloat16


def bf(x):
    return np.asarray(x, np.float32).astype(BF16)


def f64(x):
    return np.asarray(x).astype(np.float64)


E2M1 = np.array([0.0, 0.5, 1.0, 1.5, 2.0, 3.0, 4.0, 6.0, -0.0, -0.5, -1.0, -1.5, -2.0, -3.0, -4.0, -6.0])


def pack_weight(w, fmt):
    k, n = w.shape
    w = f64(bf(w)).reshape(k // 32, 32, n)
    amax = np.abs(w).max(1)
    if fmt == "e4m3":
        byte = np.frexp(amax)[1] - 1 + 127 - 7
    else:
        mant, ex = np.frexp(amax / 6.0)
        byte = np.where(mant > 0.5, ex, ex - 1) + 127
    byte = np.clip(np.where(amax > 0, byte, 1), 1, 254)
    scaled = (w * np.exp2(127.0 - byte)[:, None, :]).reshape(k, n).astype(np.float32)
    by_word = np.ascontiguousarray(scaled.reshape(k // 512, 128, 4, n).transpose(0, 1, 3, 2))
    if fmt == "e4m3":
        words = by_word.astype(ml_dtypes.float8_e4m3fn).view(np.uint8)
    else:
        c = by_word.astype(ml_dtypes.float4_e2m1fn).view(np.uint8) & 0xF
        words = c[..., 0::2] | (c[..., 1::2] << 4)
    return np.ascontiguousarray(words), np.ascontiguousarray(byte.astype(np.uint8).reshape(k // 512, 16, n))


def unpack_weight(words, scales, fmt):
    g, p, n, _ = words.shape
    if fmt == "e4m3":
        vals = np.ascontiguousarray(words).view(ml_dtypes.float8_e4m3fn).astype(np.float64)
    else:
        nib = np.empty((g, p, n, 4), np.uint8)
        nib[..., 0::2] = words & 0xF
        nib[..., 1::2] = words >> 4
        vals = E2M1[nib]
    vals = vals * np.repeat(np.exp2(scales.astype(np.float64) - 127.0), 8, axis=1)[..., None]
    return vals.transpose(0, 1, 3, 2).reshape(g * 512, n)

E4M3FN = np.array([(-1.0 if i & 128 else 1.0) * ((1.0 + (i & 7) / 8.0) * 2.0 ** (((i >> 3) & 15) - 7) if i & 120 else (i & 7) * 2.0 ** -9) for i in range(256)])


def e4m3fn_bytes(y):
    return np.clip(np.asarray(y, np.float64), -448.0, 448.0).astype(np.float32).astype(ml_dtypes.float8_e4m3fn).view(np.uint8)


def e4m3fn_values(b):
    return E4M3FN[b]


B, T, D, N, E = 2, 1024, 1024, 512, 1024


def softplus(z):
    return np.maximum(z, 0.0) + np.log1p(np.exp(-np.abs(z)))


def sigmoid(z):
    return 1.0 / (1.0 + np.exp(-z))


def draw0():
    s = mx_kscale(D)
    t = mx_kscale(T)
    x = bf(np.random.standard_normal((B, T, D)) * s)
    wg_words, wg_scales = pack_weight(np.random.standard_normal((D, N)) / np.sqrt(D) / s[:, None], "e4m3")
    bg = bf(0.5 * np.random.standard_normal(N))
    wt_words, wt_scales = pack_weight(1.5 * np.random.standard_normal((D, N)) / np.sqrt(D) / s[:, None], "e4m3")
    return {
        "x": x,
        "wg_words": wg_words,
        "wg_scales": wg_scales,
        "bg": bg,
        "wt_words": wt_words,
        "wt_scales": wt_scales,
        "k": bf(np.random.standard_normal((B, T, N)) * t[:, None]),
        "v": bf(np.random.standard_normal((B, T, E)) / np.sqrt(T) / t[:, None]),
        "s0": bf(np.random.standard_normal((B, N, E))),
    }


def core(x, wg_words, wg_scales, bg, wt_words, wt_scales, k, v, s0):
    steps = x.shape[1]
    xq = mxq(f64(x), 2, "e4m3")
    g = softplus((xq @ unpack_weight(wg_words, wg_scales, "e4m3")) + f64(bg))
    tau = sigmoid(xq @ unpack_weight(wt_words, wt_scales, "e4m3"))
    kw = np.exp(tau * np.log(g)) * f64(k)
    dec = np.exp(-(1.0 / steps) * np.sum(g * tau, axis=1))
    kwq = mxq(kw, 1, "e4m3")
    wr = kwq.transpose(0, 2, 1) @ mxq(f64(v), 1, "e4m3")
    return dec[:, :, None] * f64(s0) + wr


def setup_inputs():
    drawn = draw0()
    full = np.asarray(drawn['x']).astype(np.float64)
    scale = (np.abs(full).reshape(2, 8, 128, 8, 128).max(axis=(2, 4)) / 448.0).astype(np.float32)
    given = {}
    for key, value in drawn.items():
        if key == 'x':
            given['x_bytes'] = e4m3fn_bytes(full / np.repeat(np.repeat(scale.astype(np.float64), 128, axis=1), 128, axis=2))
            given['x_scale'] = scale
        else:
            given[key] = value
    return given


def reference(x_bytes, x_scale, wg_words, wg_scales, bg, wt_words, wt_scales, k, v, s0):
    return core(e4m3fn_values(x_bytes) * np.repeat(np.repeat(x_scale.astype(np.float64), 128, axis=1), 128, axis=2), wg_words, wg_scales, bg, wt_words, wt_scales, k, v, s0)

@@ -1,0 +1,519 @@
+from contextlib import ExitStack
+
+import concourse.mybir as mybir
+from concourse.masks import make_identity
+
+F32 = mybir.dt.float32
+BF16 = mybir.dt.bfloat16
+I32 = mybir.dt.int32
+U32 = mybir.dt.uint32
+U8 = mybir.dt.uint8
+FP8 = mybir.dt.float8_e4m3fn
+FP8X4 = mybir.dt.float8_e4m3fn_x4
+ACT = mybir.ActivationFunctionType
+ALU = mybir.AluOpType
+
+B, T, D, N, E = 2, 1024, 1024, 512, 1024
+P = 128
+J = 4
+CH = 512
+FLOPS = 2 * (2 * B * T * D * N) + 2 * B * T * N * E
+
+EXACT_ABOVE = 20.0
+LOG_BELOW = -8.0
+
+
+def tile_rodimustemperedgatestatewrite_d2p_kernel(
+    tc, x_bytes, x_scale, wg_words, wg_scales, bg, wt_words, wt_scales, k, v, s0, out
+):
+    nc = tc.nc
+    with ExitStack() as ctx:
+        pool = ctx.enter_context(tc.tile_pool(name="sb", bufs=1))
+        psum = ctx.enter_context(tc.psum_pool(name="ps", bufs=1))
+        ctx.enter_context(tc.manual_schedule())
+
+        chunks = [(b, g) for b in range(B) for g in range(2)]
+        xb, vraw, kt, wr = {}, {}, {}, {}
+
+        def buffers(name, count, shape, dtype):
+            return [pool.tile(shape, dtype, name="%s%d" % (name, i), align_bytes=64) for i in range(count)]
+
+        def banks(name, count):
+            return [psum.tile([P, 512], F32, name="%s%d" % (name, i)) for i in range(count)]
+
+        xb_buf = buffers("xb", 2, [P, J, D], U8)
+        xw_buf = buffers("xw", 4, [P, 2, D], BF16)
+        xg_buf = buffers("xg", 3, [P, 4 * CH], BF16)
+        xq_buf = buffers("xq", 2, [P, 2, CH], U32)
+        xqs_buf = buffers("xqs", 2, [P, 2, CH], U8)
+        zb_buf = buffers("zb", 3, [P, J, N], F32)
+        gt_buf = buffers("gt", 3, [P, J, N], F32)
+        th_buf = buffers("th", 3, [P, J, 4, 130], F32)
+        lg_buf = buffers("lg", 2, [P, 2, N], F32)
+        kt_buf = buffers("kt", 3, [P, J, N], BF16)
+        kwg_buf = buffers("kwg", 3, [P, 256, J], BF16)
+        kwq_buf = buffers("kwq", 4, [P, N], U32)
+        kwqs_buf = buffers("kwqs", 4, [P, N], U8)
+        vraw_buf = buffers("vraw", 4, [P, J, 512], BF16)
+        vg_buf = buffers("vg", 2, [P, 512, J], BF16)
+        vq_buf = buffers("vq", 4, [P, E], U32)
+        vqs_buf = buffers("vqs", 4, [P, E], U8)
+        s0_buf = buffers("s0t", 2, [P, 2, E], BF16)
+        ot_buf = buffers("ot", 2, [P, E], F32)
+        acc = buffers("acc", 2, [P, 4], F32)
+        dec = buffers("dec", 2, [P, 4], F32)
+        md_buf = buffers("md", 2, [P, 130], F32)
+        xt_bank = banks("xt", 2)
+        zg_bank = banks("zg", 2)
+        zt_bank = banks("zt", 2)
+        wr_bank = banks("wr", 2)
+        for t in th_buf:
+            nc.gpsimd.memset(t[:, :, :, 128:130], 1.0)
+
+        def load_x(c):
+            b, g = chunks[c]
+            xb[c] = xb_buf[c % 2]
+            src = x_bytes[b, CH * g : CH * (g + 1), :].rearrange("(p j) d -> p j d", j=J)
+            for h in range(2):
+                nc.sync.dma_start(out=xb[c][:, 2 * h : 2 * h + 2, :], in_=src[:, 2 * h : 2 * h + 2, :])
+
+        def load_k(c):
+            b, g = chunks[c]
+            kt[c] = kt_buf[c % 3]
+            nc.sync.dma_start(out=kt[c][:], in_=k[b, CH * g : CH * (g + 1), :].rearrange("(p j) n -> p j n", j=J))
+
+        def load_v(c, h):
+            b, g = chunks[c]
+            vraw[c, h] = vraw_buf[(2 * c + h) % 4]
+            src = v[b, CH * g : CH * (g + 1), 512 * h : 512 * h + 512].rearrange("(p j) e -> p j e", j=J)
+            nc.sync.dma_start(out=vraw[c, h][:], in_=src)
+
+        load_x(0)
+        xs = pool.tile([P, B, 2, 8], F32, name="xs")
+        xs_src = x_scale.rearrange("b (g q) i -> q b g i", q=4)
+        for q in range(4):
+            nc.scalar.dma_start(out=xs[32 * q : 32 * q + 32, :, :, :], in_=xs_src[q].partition_broadcast(32))
+        ident = pool.tile([P, P], F32, name="ident")
+        make_identity(nc, ident[:])
+        ws = pool.tile([P, N], U8, name="ws", align_bytes=64)
+        nc.vector.memset(ws[:].bitcast(I32), 0)
+        brow = pool.tile([P, N], BF16, name="brow")
+        nc.vector.memset(brow[:], 0.0)
+        ones = pool.tile([P, P], BF16, name="ones")
+        nc.vector.memset(ones[:], 1.0)
+        nc.scalar.dma_start(out=brow[0:1, :], in_=bg.rearrange("(o n) -> o n", o=1))
+        wq = [pool.tile([P, 2, N], I32, name="wq%d" % w, align_bytes=64) for w in range(2)]
+        for g in range(2):
+            for w, words in enumerate((wg_words, wt_words)):
+                nc.sync.dma_start(out=wq[w][:, g, :], in_=words[g].rearrange("p n t -> p (n t)").bitcast(I32))
+        load_x(1)
+        for g in range(2):
+            for w, scl in enumerate((wg_scales, wt_scales)):
+                k0 = 4 * (2 * w + g)
+                for q in range(4):
+                    nc.sync.dma_start(
+                        out=ws[32 * q + k0 : 32 * q + k0 + 4, :].bitcast(I32),
+                        in_=scl[g, 4 * q : 4 * q + 4, :].bitcast(I32),
+                    )
+        mask = pool.tile([P, 130], F32, name="mask")
+        nc.vector.memset(mask[:, 128:130], 0.5)
+        nc.vector.tensor_copy(out=mask[:, 0:128], in_=ident[:])
+        bias = pool.tile([P, N], F32, name="bias")
+
+        def load_bias():
+            wr["bias"] = wr_bank[0]
+            nc.tensor.matmul(wr["bias"][:], lhsT=ones[:], rhs=brow[:], start=True, stop=True)
+
+        def keep_bias():
+            nc.scalar.copy(out=bias[:], in_=wr["bias"][:])
+
+        xw, xt, xg, xq, xqs = {}, {}, {}, {}, {}
+
+        def widen(c, s, jj, eng):
+            b, g = chunks[c]
+            h, gp = divmod(s, 2)
+            xw[c, h] = xw_buf[(2 * c + h) % 4]
+            for i in range(4 * gp, 4 * gp + 4):
+                o = xw[c, h][:, jj, 128 * i : 128 * i + 128]
+                a = xb[c][:, 2 * h + jj, 128 * i : 128 * i + 128].bitcast(FP8)
+                sc = xs[:, b, g, i : i + 1]
+                if eng == "A":
+                    nc.any.tensor_scalar(out=o, in0=a, scalar1=sc, scalar2=None, op0=ALU.mult)
+                elif eng == "S":
+                    nc.scalar.activation(out=o, in_=a, func=ACT.Copy, scale=sc)
+                else:
+                    nc.vector.tensor_scalar(out=o, in0=a, scalar1=sc, scalar2=None, op0=ALU.mult)
+
+        def copy(eng, out, in_):
+            if eng == "A":
+                nc.any.tensor_copy(out=out, in_=in_)
+            elif eng == "S":
+                nc.scalar.copy(out=out, in_=in_)
+            else:
+                nc.vector.tensor_copy(out=out, in_=in_)
+
+        def turn_x(c, s):
+            h, gp = divmod(s, 2)
+            xt[c, s] = xt_bank[s % 2][:].rearrange("p (u r) -> p u r", u=2)
+            for jj in range(2):
+                wv = xw[c, h][:, jj, :].bitcast(F32)
+                for u in range(2):
+                    nc.tensor.transpose(
+                        xt[c, s][:, u, 128 * jj : 128 * jj + 128], wv[:, 256 * gp + u : 256 * gp + 256 : 2], ident[:]
+                    )
+
+        def empty_x(c, s, eng):
+            h, gp = divmod(s, 2)
+            xg[c, gp] = xg_buf[(2 * c + gp) % 3]
+            copy(
+                eng,
+                out=xg[c, gp][:, 1024 * h : 1024 * h + 1024].bitcast(F32).rearrange("p (r u) -> p r u", u=2),
+                in_=xt[c, s].rearrange("p u r -> p r u"),
+            )
+
+        def quant_x(c, gp):
+            xq[c], xqs[c] = xq_buf[c % 2], xqs_buf[c % 2]
+            nc.vector.quantize_mx(out=xq[c][:, gp, :].bitcast(FP8X4), scales=xqs[c][:, gp, :], in_=xg[c, gp][:])
+
+        zb, gt, zz, th = {}, {}, {}, {}
+
+        def gate_mm(c, j):
+            for w in range(2):
+                z = (zg_bank, zt_bank)[w][j % 2]
+                zz[c, j, w] = z
+                for gp in range(2):
+                    k0 = 4 * (2 * w + gp)
+                    nc.tensor.matmul_mx(
+                        out=z[:],
+                        lhsT=xq[c][:, gp, 128 * j : 128 * j + 128].bitcast(FP8X4),
+                        lhsT_scale=xqs[c][:, gp, 128 * j : 128 * j + 128],
+                        rhs=wq[w][:, gp, :].bitcast(FP8X4),
+                        rhs_scale=ws[k0:128, :],
+                        start=(gp == 0),
+                        stop=(gp == 1),
+                    )
+
+        def add_bias(c, j):
+            zb[c] = zb_buf[c % 3]
+            nc.vector.tensor_tensor(out=zb[c][:, j, :], in0=zz[c, j, 0][:], in1=bias[:], op=ALU.add)
+
+        def tau(c, j):
+            th[c] = th_buf[c % 3]
+            nc.scalar.activation(
+                out=th[c][:, j, :, 0:128], in_=zz[c, j, 1][:].rearrange("p (t n) -> p t n", t=4), func=ACT.Tanh, scale=0.5
+            )
+
+        def exp_z(i):
+            c, h = divmod(i, 2)
+            gt[c] = gt_buf[c % 3]
+            s = slice(2 * h, 2 * h + 2)
+            nc.scalar.activation(out=gt[c][:, s, :], in_=zb[c][:, s, :], func=ACT.Exp)
+
+        vg, vq, vqs = {}, {}, {}
+
+        def turn_v(c, h, eng):
+            vg[c, h] = vg_buf[h]
+            copy(
+                eng,
+                out=vg[c, h][:].rearrange("p (c i) j -> p c j i", i=4),
+                in_=vraw[c, h][:].rearrange("p j (c i) -> p c j i", i=4),
+            )
+
+        def quant_v(c, h):
+            vq[c], vqs[c] = vq_buf[c], vqs_buf[c]
+            e = slice(512 * h, 512 * h + 512)
+            nc.vector.quantize_mx(
+                out=vq[c][:, e].bitcast(FP8X4), scales=vqs[c][:, e], in_=vg[c, h][:].rearrange("p e j -> p (e j)")
+            )
+
+        def softplus_log(i):
+            c, h = divmod(i, 2)
+            s = slice(2 * h, 2 * h + 2)
+            nc.scalar.activation(out=gt[c][:, s, :], in_=gt[c][:, s, :], func=ACT.Ln, bias=1.0)
+
+        def softplus_large(i):
+            c, h = divmod(i, 2)
+            s = slice(2 * h, 2 * h + 2)
+            nc.vector.scalar_tensor_tensor(
+                out=gt[c][:, s, :], in0=gt[c][:, s, :], scalar=EXACT_ABOVE, in1=zb[c][:, s, :], op0=ALU.min, op1=ALU.max
+            )
+
+        lg = {}
+
+        def gate_log(i):
+            c, h = divmod(i, 2)
+            lg[i] = lg_buf[i % 2]
+            nc.scalar.activation(out=lg[i][:], in_=gt[c][:, 2 * h : 2 * h + 2, :], func=ACT.Ln)
+
+        def log_small(i):
+            c, h = divmod(i, 2)
+            s = slice(2 * h, 2 * h + 2)
+            nc.vector.scalar_tensor_tensor(
+                out=zb[c][:, s, :], in0=lg[i][:], scalar=LOG_BELOW, in1=zb[c][:, s, :], op0=ALU.max, op1=ALU.min
+            )
+
+        def exponent(i):
+            c, h = divmod(i, 2)
+            s = slice(2 * h, 2 * h + 2)
+            zv = zb[c][:, s, :].rearrange("p j (t n) -> p j t n", t=4)
+            nc.vector.scalar_tensor_tensor(
+                out=zv, in0=th[c][:, s, :, 0:128], scalar=1.0, in1=zv, op0=ALU.add, op1=ALU.mult
+            )
+
+        dg = {}
+
+        def decay_mm(b, pair):
+            dg[b, pair] = wr_bank[pair][:, 0:260].rearrange("p (q n) -> p q n", q=2)
+            units = [(2 * b + g, j) for g in range(2) for j in range(J)]
+            for q in range(2):
+                nt = 2 * pair + q
+                for n, (c, j) in enumerate(units):
+                    nc.tensor.matmul(
+                        dg[b, pair][:, q, :],
+                        lhsT=gt[c][:, j, 128 * nt : 128 * nt + 128],
+                        rhs=th[c][:, j, nt, :],
+                        start=(n == 0),
+                        stop=(n == len(units) - 1),
+                    )
+
+        def decay_sum(b, pair):
+            for q in range(2):
+                nt = 2 * pair + q
+                nc.vector.scalar_tensor_tensor(
+                    out=md_buf[q][:],
+                    in0=dg[b, pair][:, q, :],
+                    scalar=1.0,
+                    in1=mask[:],
+                    op0=ALU.mult,
+                    op1=ALU.mult,
+                    accum_out=acc[b][:, nt : nt + 1],
+                )
+
+        def decay_exp(b):
+            nc.scalar.activation(out=dec[b][:], in_=acc[b][:], func=ACT.Exp, scale=-0.5 / T)
+
+        kwq, kwqs, kwg = {}, {}, {}
+
+        def tempered(c, h):
+            n = slice(256 * h, 256 * h + 256)
+            nc.scalar.activation(out=zb[c][:, :, n], in_=zb[c][:, :, n], func=ACT.Exp, scale=0.5)
+
+        def weigh(c, h):
+            n = slice(256 * h, 256 * h + 256)
+            kwg[c, h] = kwg_buf[(2 * c + h) % 3]
+            nc.vector.tensor_tensor(
+                out=kwg[c, h][:].rearrange("p (c i) j -> p c j i", i=4),
+                in0=zb[c][:, :, n].rearrange("p j (c i) -> p c j i", i=4),
+                in1=kt[c][:, :, n].rearrange("p j (c i) -> p c j i", i=4),
+                op=ALU.mult,
+            )
+
+        def quant_kw(c, h):
+            n = slice(256 * h, 256 * h + 256)
+            kwq[c], kwqs[c] = kwq_buf[c], kwqs_buf[c]
+            nc.vector.quantize_mx(
+                out=kwq[c][:, n].bitcast(FP8X4), scales=kwqs[c][:, n], in_=kwg[c, h][:].rearrange("p n j -> p (n j)")
+            )
+
+        s0t, ot = {}, {}
+
+        def load_s0(b, pair):
+            s0t[b, pair] = s0_buf[pair]
+            nc.sync.dma_start(
+                out=s0t[b, pair][:], in_=s0[b, 256 * pair : 256 * pair + 256, :].rearrange("(q p) e -> p q e", p=P)
+            )
+
+        def write_mm(b, nt, eh):
+            wr[b, nt, eh] = (xt_bank if b == 0 else (zg_bank, zt_bank)[nt % 2])[eh]
+            e = slice(512 * eh, 512 * eh + 512)
+            n = slice(128 * nt, 128 * nt + 128)
+            for g in range(2):
+                c = 2 * b + g
+                nc.tensor.matmul_mx(
+                    out=wr[b, nt, eh][:],
+                    lhsT=kwq[c][:, n].bitcast(FP8X4),
+                    lhsT_scale=kwqs[c][:, n],
+                    rhs=vq[c][:, e].bitcast(FP8X4),
+                    rhs_scale=vqs[c][:, e],
+                    start=(g == 0),
+                    stop=(g == 1),
+                )
+
+        def finish(b, nt, eh):
+            ot[b, nt] = ot_buf[nt % 2][:] if nt < 2 else xg_buf[nt % 2][:].bitcast(F32)
+            e = slice(512 * eh, 512 * eh + 512)
+            nc.vector.scalar_tensor_tensor(
+                out=ot[b, nt][:, e],
+                in0=s0t[b, nt // 2][:, nt % 2, e],
+                scalar=dec[b][:, nt : nt + 1],
+                in1=wr[b, nt, eh][:],
+                op0=ALU.mult,
+                op1=ALU.add,
+            )
+
+        def store(b, nt):
+            nc.sync.dma_start(out=out[b, P * nt : P * nt + P, :], in_=ot[b, nt])
+
+        def run(fn, *args):
+            fn(*args)
+
+
+        for s in range(5):
+            if s < 4:
+                run(widen, 0, s, 0, "V")
+                run(widen, 0, s, 1, "S")
+                run(turn_x, 0, s)
+            if s > 0:
+                run(empty_x, 0, s - 1, "V")
+        run(load_bias)
+        run(load_x, 2)
+        run(load_v, 0, 0)
+        run(load_v, 0, 1)
+        for s in range(4):
+            run(widen, 1, s, 0, "V")
+            run(widen, 1, s, 1, "V" if s else "S")
+            run(turn_x, 1, s)
+            if s == 0:
+                run(keep_bias)
+            if s < 2:
+                run(quant_x, 0, s)
+            run(empty_x, 1, s, "S")
+        run(load_x, 3)
+        run(load_v, 1, 0)
+        run(load_v, 1, 1)
+        for c in range(3):
+            run(load_k, c)
+        run(load_s0, 0, 0)
+        run(load_s0, 0, 1)
+        for c in range(2):
+            for j in range(4):
+                run(gate_mm, c, j)
+                run(widen, c + 2, j, 0, "V")
+                run(widen, c + 2, j, 1, "V")
+                run(add_bias, c, j)
+                run(tau, c, j)
+                if j % 2:
+                    run(exp_z, 2 * c + j // 2)
+                if c == 0 and j < 2:
+                    run(quant_x, 1, j)
+                if c == 1:
+                    run(turn_x, 2, j)
+                    run(empty_x, 2, j, "S")
+        for i in range(5):
+            if i < 4:
+                run(softplus_log, i)
+                run(turn_x, 3, i)
+            if i > 0:
+                run(empty_x, 3, i - 1, "S")
+            if i < 2:
+                run(turn_v, 0, i, "V")
+                run(quant_x, 2, i)
+            if i in (1, 2):
+                run(gate_mm, 2, i - 1)
+            if i > 0:
+                run(softplus_large, i - 1)
+            if i in (2, 3):
+                run(quant_v, 0, i - 2)
+        run(load_v, 2, 0)
+        run(load_v, 2, 1)
+        run(decay_mm, 0, 0)
+        for i in range(6):
+            if i < 4:
+                run(gate_log, i)
+            if i == 1:
+                run(turn_v, 1, 0, "S")
+            if i in (0, 1):
+                run(add_bias, 2, i)
+                run(quant_x, 3, i)
+            if 1 <= i < 5:
+                run(log_small, i - 1)
+            if i >= 2:
+                run(exponent, i - 2)
+        run(turn_v, 1, 1, "S")
+        ks = [(0, 0), (0, 1), (1, 0), (1, 1)]
+        for i in range(4):
+            run(tau, 2, i)
+            if i < 2:
+                run(gate_mm, 2, i + 2)
+                run(add_bias, 2, i + 2)
+            if i == 1:
+                run(decay_mm, 0, 1)
+            if i >= 1:
+                run(tempered, *ks[i - 1])
+                run(weigh, *ks[i - 1])
+            if i < 2:
+                run(quant_v, 1, i)
+            if i >= 2:
+                run(quant_kw, *ks[i - 2])
+        run(exp_z, 4)
+        run(tempered, *ks[3])
+        for j in range(2):
+            run(gate_mm, 3, j)
+            run(add_bias, 3, j)
+        run(weigh, *ks[3])
+        run(exp_z, 5)
+        for i in (2, 3):
+            run(quant_kw, *ks[i])
+        for j in range(4):
+            run(tau, 3, j)
+            if j < 2:
+                run(gate_mm, 3, j + 2)
+                run(add_bias, 3, j + 2)
+            if j % 2:
+                run(exp_z, 6 + j // 2)
+        run(load_k, 3)
+        for pair in range(2):
+            run(decay_sum, 0, pair)
+        run(decay_exp, 0)
+        run(load_v, 3, 0)
+        run(load_v, 3, 1)
+        outs = [(nt, eh) for nt in range(4) for eh in range(2)]
+        vs = [(2, 0), (2, 1), (3, 0), (3, 1)]
+        for i in range(4):
+            run(softplus_log, 4 + i)
+            if i in (1, 3):
+                run(turn_v, *vs[i // 2], "S")
+            for q in range(2):
+                run(write_mm, 0, *outs[2 * i + q])
+            for q in range(2):
+                run(finish, 0, *outs[2 * i + q])
+            run(store, 0, i)
+            if i % 2:
+                run(load_s0, 1, i // 2)
+            if i > 0:
+                run(softplus_large, 3 + i)
+        run(softplus_large, 7)
+        for h in range(2):
+            run(quant_v, 2, h)
+        for pair in range(2):
+            run(decay_mm, 1, pair)
+        for i in range(6):
+            if i < 4:
+                run(gate_log, 4 + i)
+            if i in (1, 2):
+                run(turn_v, 3, i - 1, "S")
+            if 1 <= i < 5:
+                run(log_small, 3 + i)
+            if i in (3, 4):
+                run(quant_v, 3, i - 3)
+            if i >= 2:
+                run(exponent, 2 + i)
+        for pair in range(2):
+            run(decay_sum, 1, pair)
+        ks = [(2, 0), (3, 0), (2, 1), (3, 1)]
+        for i in range(6):
+            if i < 4:
+                run(tempered, *ks[i])
+            if i == 3:
+                run(decay_exp, 1)
+            if 1 <= i < 5:
+                run(weigh, *ks[i - 1])
+            if i >= 2:
+                run(quant_kw, *ks[i - 2])
+        for i in range(9):
+            if i < 8:
+                run(write_mm, 1, *outs[i])
+            if i > 0:
+                run(finish, 1, *outs[i - 1])
+                if i % 2 == 0:
+                    run(store, 1, i // 2 - 1)

@@ -101,6 +101,8 @@ def tile_rodimustemperedgatestatewrite_d2p_kernel(
         nc.vector.memset(brow[:], 0.0)
         ones = pool.tile([P, P], BF16, name="ones")
         nc.vector.memset(ones[:], 1.0)
+        eye = pool.tile([P, P], BF16, name="eye")
+        nc.vector.tensor_copy(out=eye[:], in_=ident[:])
         nc.scalar.dma_start(out=brow[0:1, :], in_=bg.rearrange("(o n) -> o n", o=1))
         wq = [pool.tile([P, 2, N], I32, name="wq%d" % w, align_bytes=64) for w in range(2)]
         for g in range(2):
@@ -219,6 +221,22 @@ def tile_rodimustemperedgatestatewrite_d2p_kernel(
                 in_=vraw[c, h][:].rearrange("p j (c i) -> p c j i", i=4),
             )
 
+        def turn_v_mm(c, h):
+            for i in range(4):
+                nc.tensor.matmul(
+                    xt_bank[i // 2][:].bitcast(BF16)[:, 512 * (i % 2) : 512 * (i % 2) + 512].rearrange("p (e j) -> p e j", j=J),
+                    lhsT=eye[:],
+                    rhs=vraw[c, h][:, :, 128 * i : 128 * i + 128].rearrange("p j e -> p e j"),
+                    start=True,
+                    stop=True,
+                )
+
+        def empty_v(c, h, eng="S"):
+            vg[c, h] = vg_buf[h]
+            flat = vg[c, h][:].rearrange("p e j -> p (e j)")
+            for i in range(2):
+                copy(eng, out=flat[:, 1024 * i : 1024 * i + 1024], in_=xt_bank[i][:].bitcast(BF16))
+
         def quant_v(c, h):
             vq[c], vqs[c] = vq_buf[c], vqs_buf[c]
             e = slice(512 * h, 512 * h + 512)
@@ -324,7 +342,7 @@ def tile_rodimustemperedgatestatewrite_d2p_kernel(
             )
 
         def write_mm(b, nt, eh):
-            wr[b, nt, eh] = (xt_bank if b == 0 else (zg_bank, zt_bank)[nt % 2])[eh]
+            wr[b, nt, eh] = (zg_bank, zt_bank)[nt % 2][eh]
             e = slice(512 * eh, 512 * eh + 512)
             n = slice(128 * nt, 128 * nt + 128)
             for g in range(2):
@@ -351,8 +369,8 @@ def tile_rodimustemperedgatestatewrite_d2p_kernel(
                 op1=ALU.add,
             )
 
-        def store(b, nt):
-            nc.sync.dma_start(out=out[b, P * nt : P * nt + P, :], in_=ot[b, nt])
+        def store(b, nt, cols=slice(0, E)):
+            nc.sync.dma_start(out=out[b, P * nt : P * nt + P, cols], in_=ot[b, nt][:, cols])
 
         def run(fn, *args):
             fn(*args)
@@ -361,10 +379,10 @@ def tile_rodimustemperedgatestatewrite_d2p_kernel(
         for s in range(5):
             if s < 4:
                 run(widen, 0, s, 0, "V")
-                run(widen, 0, s, 1, "S")
+                run(widen, 0, s, 1, "V" if s > 1 else "S")
                 run(turn_x, 0, s)
             if s > 0:
-                run(empty_x, 0, s - 1, "V")
+                run(empty_x, 0, s - 1, "S")
         run(load_bias)
         run(load_x, 2)
         run(load_v, 0, 0)
@@ -416,12 +434,13 @@ def tile_rodimustemperedgatestatewrite_d2p_kernel(
                 run(quant_v, 0, i - 2)
         run(load_v, 2, 0)
         run(load_v, 2, 1)
+        run(turn_v_mm, 1, 0)
         run(decay_mm, 0, 0)
         for i in range(6):
             if i < 4:
                 run(gate_log, i)
             if i == 1:
-                run(turn_v, 1, 0, "S")
+                run(empty_v, 1, 0)
             if i in (0, 1):
                 run(add_bias, 2, i)
                 run(quant_x, 3, i)
@@ -429,7 +448,8 @@ def tile_rodimustemperedgatestatewrite_d2p_kernel(
                 run(log_small, i - 1)
             if i >= 2:
                 run(exponent, i - 2)
-        run(turn_v, 1, 1, "S")
+        run(turn_v_mm, 1, 1)
+        run(empty_v, 1, 1)
         ks = [(0, 0), (0, 1), (1, 0), (1, 1)]
         for i in range(4):
             run(tau, 2, i)
@@ -472,7 +492,8 @@ def tile_rodimustemperedgatestatewrite_d2p_kernel(
         for i in range(4):
             run(softplus_log, 4 + i)
             if i in (1, 3):
-                run(turn_v, *vs[i // 2], "S")
+                run(turn_v_mm, *vs[i // 2])
+                run(empty_v, *vs[i // 2])
             for q in range(2):
                 run(write_mm, 0, *outs[2 * i + q])
             for q in range(2):
@@ -485,13 +506,16 @@ def tile_rodimustemperedgatestatewrite_d2p_kernel(
         run(softplus_large, 7)
         for h in range(2):
             run(quant_v, 2, h)
-        for pair in range(2):
-            run(decay_mm, 1, pair)
         for i in range(6):
             if i < 4:
                 run(gate_log, 4 + i)
-            if i in (1, 2):
-                run(turn_v, 3, i - 1, "S")
+            if i == 1:
+                run(turn_v_mm, 3, 0)
+                run(empty_v, 3, 0)
+            if i in (2, 3):
+                run(decay_mm, 1, i - 2)
+            if i == 2:
+                run(turn_v, 3, 1, "S")
             if 1 <= i < 5:
                 run(log_small, 3 + i)
             if i in (3, 4):
@@ -514,6 +538,9 @@ def tile_rodimustemperedgatestatewrite_d2p_kernel(
             if i < 8:
                 run(write_mm, 1, *outs[i])
             if i > 0:
-                run(finish, 1, *outs[i - 1])
-                if i % 2 == 0:
-                    run(store, 1, i // 2 - 1)
+                nt, eh = outs[i - 1]
+                run(finish, 1, nt, eh)
+                if nt == 3:
+                    run(store, 1, nt, slice(512 * eh, 512 * eh + 512))
+                elif eh:
+                    run(store, 1, nt)

@@ -49,7 +49,8 @@ def tile_rodimustemperedgatestatewrite_d2p_kernel(
         zb_buf = buffers("zb", 3, [P, J, N], F32)
         gt_buf = buffers("gt", 3, [P, J, N], F32)
         th_buf = buffers("th", 3, [P, J, 4, 130], F32)
-        lg_buf = buffers("lg", 2, [P, 2, N], F32)
+        lg_buf = buffers("lg", 2, [P, J, N], F32)
+        ot_buf = [lg_buf[1][:, 2 * i : 2 * i + 2, :].rearrange("p j n -> p (j n)") for i in range(2)]
         kt_buf = buffers("kt", 3, [P, J, N], BF16)
         kwg_buf = buffers("kwg", 3, [P, 256, J], BF16)
         kwq_buf = buffers("kwq", 4, [P, N], U32)
@@ -59,7 +60,6 @@ def tile_rodimustemperedgatestatewrite_d2p_kernel(
         vq_buf = buffers("vq", 4, [P, E], U32)
         vqs_buf = buffers("vqs", 4, [P, E], U8)
         s0_buf = buffers("s0t", 2, [P, 2, E], BF16)
-        ot_buf = buffers("ot", 2, [P, E], F32)
         acc = buffers("acc", 2, [P, 4], F32)
         dec = buffers("dec", 2, [P, 4], F32)
         md_buf = buffers("md", 2, [P, 130], F32)
@@ -70,12 +70,13 @@ def tile_rodimustemperedgatestatewrite_d2p_kernel(
         for t in th_buf:
             nc.gpsimd.memset(t[:, :, :, 128:130], 1.0)
 
-        def load_x(c):
+        def load_x(c, parts=1):
             b, g = chunks[c]
             xb[c] = xb_buf[c % 2]
             src = x_bytes[b, CH * g : CH * (g + 1), :].rearrange("(p j) d -> p j d", j=J)
-            for h in range(2):
-                nc.sync.dma_start(out=xb[c][:, 2 * h : 2 * h + 2, :], in_=src[:, 2 * h : 2 * h + 2, :])
+            r = J // parts
+            for h in range(parts):
+                nc.sync.dma_start(out=xb[c][:, r * h : r * h + r, :], in_=src[:, r * h : r * h + r, :])
 
         def load_k(c):
             b, g = chunks[c]
@@ -88,15 +89,18 @@ def tile_rodimustemperedgatestatewrite_d2p_kernel(
             src = v[b, CH * g : CH * (g + 1), 512 * h : 512 * h + 512].rearrange("(p j) e -> p j e", j=J)
             nc.sync.dma_start(out=vraw[c, h][:], in_=src)
 
-        load_x(0)
+        load_x(0, 2)
         xs = pool.tile([P, B, 2, 8], F32, name="xs")
         xs_src = x_scale.rearrange("b (g q) i -> q b g i", q=4)
         for q in range(4):
             nc.scalar.dma_start(out=xs[32 * q : 32 * q + 32, :, :, :], in_=xs_src[q].partition_broadcast(32))
         ident = pool.tile([P, P], F32, name="ident")
         make_identity(nc, ident[:])
-        ws = pool.tile([P, N], U8, name="ws", align_bytes=64)
-        nc.vector.memset(ws[:].bitcast(I32), 0)
+        ws = pool.tile([P, 4, N], U8, name="ws", align_bytes=64)
+        nc.gpsimd.memset(ws[:].rearrange("p i n -> p (i n)").bitcast(I32), 0)
+        warm = pool.tile([P, 1], F32, name="warm")
+        nc.vector.memset(warm[:], 0.0)
+        nc.scalar.activation(out=warm[:], in_=warm[:], func=ACT.Tanh)
         brow = pool.tile([P, N], BF16, name="brow")
         nc.vector.memset(brow[:], 0.0)
         ones = pool.tile([P, P], BF16, name="ones")
@@ -105,18 +109,15 @@ def tile_rodimustemperedgatestatewrite_d2p_kernel(
         nc.vector.tensor_copy(out=eye[:], in_=ident[:])
         nc.scalar.dma_start(out=brow[0:1, :], in_=bg.rearrange("(o n) -> o n", o=1))
         wq = [pool.tile([P, 2, N], I32, name="wq%d" % w, align_bytes=64) for w in range(2)]
-        for g in range(2):
-            for w, words in enumerate((wg_words, wt_words)):
-                nc.sync.dma_start(out=wq[w][:, g, :], in_=words[g].rearrange("p n t -> p (n t)").bitcast(I32))
-        load_x(1)
-        for g in range(2):
-            for w, scl in enumerate((wg_scales, wt_scales)):
-                k0 = 4 * (2 * w + g)
-                for q in range(4):
-                    nc.sync.dma_start(
-                        out=ws[32 * q + k0 : 32 * q + k0 + 4, :].bitcast(I32),
-                        in_=scl[g, 4 * q : 4 * q + 4, :].bitcast(I32),
-                    )
+        load_x(1, 2)
+        for w, words in enumerate((wg_words, wt_words)):
+            nc.sync.dma_start(out=wq[w][:], in_=words.rearrange("g p n t -> p g (n t)").bitcast(I32))
+        for w, scl in enumerate((wg_scales, wt_scales)):
+            for q in range(4):
+                nc.sync.dma_start(
+                    out=ws[32 * q : 32 * q + 4, 2 * w : 2 * w + 2, :].bitcast(I32),
+                    in_=scl[:, 4 * q : 4 * q + 4, :].rearrange("g r n -> r g n").bitcast(I32),
+                )
         mask = pool.tile([P, 130], F32, name="mask")
         nc.vector.memset(mask[:, 128:130], 0.5)
         nc.vector.tensor_copy(out=mask[:, 0:128], in_=ident[:])
@@ -179,18 +180,20 @@ def tile_rodimustemperedgatestatewrite_d2p_kernel(
 
         zb, gt, zz, th = {}, {}, {}, {}
 
+        def part(h):
+            return slice(2 * h[0], 2 * h[0] + 2) if h else slice(0, J)
+
         def gate_mm(c, j):
             for w in range(2):
                 z = (zg_bank, zt_bank)[w][j % 2]
                 zz[c, j, w] = z
                 for gp in range(2):
-                    k0 = 4 * (2 * w + gp)
                     nc.tensor.matmul_mx(
                         out=z[:],
                         lhsT=xq[c][:, gp, 128 * j : 128 * j + 128].bitcast(FP8X4),
                         lhsT_scale=xqs[c][:, gp, 128 * j : 128 * j + 128],
                         rhs=wq[w][:, gp, :].bitcast(FP8X4),
-                        rhs_scale=ws[k0:128, :],
+                        rhs_scale=ws[:, 2 * w + gp, :],
                         start=(gp == 0),
                         stop=(gp == 1),
                     )
@@ -205,10 +208,9 @@ def tile_rodimustemperedgatestatewrite_d2p_kernel(
                 out=th[c][:, j, :, 0:128], in_=zz[c, j, 1][:].rearrange("p (t n) -> p t n", t=4), func=ACT.Tanh, scale=0.5
             )
 
-        def exp_z(i):
-            c, h = divmod(i, 2)
+        def exp_z(c, *h):
             gt[c] = gt_buf[c % 3]
-            s = slice(2 * h, 2 * h + 2)
+            s = part(h)
             nc.scalar.activation(out=gt[c][:, s, :], in_=zb[c][:, s, :], func=ACT.Exp)
 
         vg, vq, vqs = {}, {}, {}
@@ -244,35 +246,30 @@ def tile_rodimustemperedgatestatewrite_d2p_kernel(
                 out=vq[c][:, e].bitcast(FP8X4), scales=vqs[c][:, e], in_=vg[c, h][:].rearrange("p e j -> p (e j)")
             )
 
-        def softplus_log(i):
-            c, h = divmod(i, 2)
-            s = slice(2 * h, 2 * h + 2)
+        def softplus_log(c, *h):
+            s = part(h)
             nc.scalar.activation(out=gt[c][:, s, :], in_=gt[c][:, s, :], func=ACT.Ln, bias=1.0)
 
-        def softplus_large(i):
-            c, h = divmod(i, 2)
-            s = slice(2 * h, 2 * h + 2)
+        def softplus_large(c, *h):
+            s = part(h)
             nc.vector.scalar_tensor_tensor(
                 out=gt[c][:, s, :], in0=gt[c][:, s, :], scalar=EXACT_ABOVE, in1=zb[c][:, s, :], op0=ALU.min, op1=ALU.max
             )
 
         lg = {}
 
-        def gate_log(i):
-            c, h = divmod(i, 2)
-            lg[i] = lg_buf[i % 2]
-            nc.scalar.activation(out=lg[i][:], in_=gt[c][:, 2 * h : 2 * h + 2, :], func=ACT.Ln)
+        def gate_log(c, *h):
+            s = part(h)
+            nc.scalar.activation(out=lg_buf[c % 2][:, s, :], in_=gt[c][:, s, :], func=ACT.Ln)
 
-        def log_small(i):
-            c, h = divmod(i, 2)
-            s = slice(2 * h, 2 * h + 2)
+        def log_small(c, *h):
+            s = part(h)
             nc.vector.scalar_tensor_tensor(
-                out=zb[c][:, s, :], in0=lg[i][:], scalar=LOG_BELOW, in1=zb[c][:, s, :], op0=ALU.max, op1=ALU.min
+                out=zb[c][:, s, :], in0=lg_buf[c % 2][:, s, :], scalar=LOG_BELOW, in1=zb[c][:, s, :], op0=ALU.max, op1=ALU.min
             )
 
-        def exponent(i):
-            c, h = divmod(i, 2)
-            s = slice(2 * h, 2 * h + 2)
+        def exponent(c, *h):
+            s = part(h)
             zv = zb[c][:, s, :].rearrange("p j (t n) -> p j t n", t=4)
             nc.vector.scalar_tensor_tensor(
                 out=zv, in0=th[c][:, s, :, 0:128], scalar=1.0, in1=zv, op0=ALU.add, op1=ALU.mult
@@ -312,8 +309,8 @@ def tile_rodimustemperedgatestatewrite_d2p_kernel(
 
         kwq, kwqs, kwg = {}, {}, {}
 
-        def tempered(c, h):
-            n = slice(256 * h, 256 * h + 256)
+        def tempered(c, *h):
+            n = slice(256 * h[0], 256 * h[0] + 256) if h else slice(0, N)
             nc.scalar.activation(out=zb[c][:, :, n], in_=zb[c][:, :, n], func=ACT.Exp, scale=0.5)
 
         def weigh(c, h):
@@ -358,7 +355,7 @@ def tile_rodimustemperedgatestatewrite_d2p_kernel(
                 )
 
         def finish(b, nt, eh):
-            ot[b, nt] = ot_buf[nt % 2][:] if nt < 2 else xg_buf[nt % 2][:].bitcast(F32)
+            ot[b, nt] = ot_buf[nt % 2] if nt < 2 else xg_buf[nt % 2][:].bitcast(F32)
             e = slice(512 * eh, 512 * eh + 512)
             nc.vector.scalar_tensor_tensor(
                 out=ot[b, nt][:, e],
@@ -369,7 +366,8 @@ def tile_rodimustemperedgatestatewrite_d2p_kernel(
                 op1=ALU.add,
             )
 
-        def store(b, nt, cols=slice(0, E)):
+        def store(b, nt, *half):
+            cols = slice(512 * half[0], 512 * half[0] + 512) if half else slice(0, E)
             nc.sync.dma_start(out=out[b, P * nt : P * nt + P, cols], in_=ot[b, nt][:, cols])
 
         def run(fn, *args):
@@ -379,7 +377,7 @@ def tile_rodimustemperedgatestatewrite_d2p_kernel(
         for s in range(5):
             if s < 4:
                 run(widen, 0, s, 0, "V")
-                run(widen, 0, s, 1, "V" if s > 1 else "S")
+                run(widen, 0, s, 1, "S" if s < 2 else "V")
                 run(turn_x, 0, s)
             if s > 0:
                 run(empty_x, 0, s - 1, "S")
@@ -389,7 +387,7 @@ def tile_rodimustemperedgatestatewrite_d2p_kernel(
         run(load_v, 0, 1)
         for s in range(4):
             run(widen, 1, s, 0, "V")
-            run(widen, 1, s, 1, "V" if s else "S")
+            run(widen, 1, s, 1, "V")
             run(turn_x, 1, s)
             if s == 0:
                 run(keep_bias)
@@ -411,15 +409,16 @@ def tile_rodimustemperedgatestatewrite_d2p_kernel(
                 run(add_bias, c, j)
                 run(tau, c, j)
                 if j % 2:
-                    run(exp_z, 2 * c + j // 2)
+                    run(exp_z, c, j // 2)
                 if c == 0 and j < 2:
                     run(quant_x, 1, j)
-                if c == 1:
-                    run(turn_x, 2, j)
-                    run(empty_x, 2, j, "S")
+                s = 4 * c + j - 2
+                if 0 <= s < 4:
+                    run(turn_x, 2, s)
+                    run(empty_x, 2, s, "S")
         for i in range(5):
             if i < 4:
-                run(softplus_log, i)
+                run(softplus_log, i // 2, i % 2)
                 run(turn_x, 3, i)
             if i > 0:
                 run(empty_x, 3, i - 1, "S")
@@ -429,7 +428,7 @@ def tile_rodimustemperedgatestatewrite_d2p_kernel(
             if i in (1, 2):
                 run(gate_mm, 2, i - 1)
             if i > 0:
-                run(softplus_large, i - 1)
+                run(softplus_large, (i - 1) // 2, (i - 1) % 2)
             if i in (2, 3):
                 run(quant_v, 0, i - 2)
         run(load_v, 2, 0)
@@ -438,16 +437,16 @@ def tile_rodimustemperedgatestatewrite_d2p_kernel(
         run(decay_mm, 0, 0)
         for i in range(6):
             if i < 4:
-                run(gate_log, i)
+                run(gate_log, i // 2, i % 2)
             if i == 1:
                 run(empty_v, 1, 0)
             if i in (0, 1):
                 run(add_bias, 2, i)
                 run(quant_x, 3, i)
             if 1 <= i < 5:
-                run(log_small, i - 1)
-            if i >= 2:
-                run(exponent, i - 2)
+                run(log_small, (i - 1) // 2, (i - 1) % 2)
+            if i in (3, 5):
+                run(exponent, i // 2 - 1)
         run(turn_v_mm, 1, 1)
         run(empty_v, 1, 1)
         ks = [(0, 0), (0, 1), (1, 0), (1, 1)]
@@ -458,20 +457,23 @@ def tile_rodimustemperedgatestatewrite_d2p_kernel(
                 run(add_bias, 2, i + 2)
             if i == 1:
                 run(decay_mm, 0, 1)
+            if i == 1:
+                run(tempered, 0)
+            if i == 3:
+                run(tempered, 1)
             if i >= 1:
-                run(tempered, *ks[i - 1])
                 run(weigh, *ks[i - 1])
             if i < 2:
                 run(quant_v, 1, i)
             if i >= 2:
                 run(quant_kw, *ks[i - 2])
-        run(exp_z, 4)
-        run(tempered, *ks[3])
+        run(exp_z, 2, 0)
+
         for j in range(2):
             run(gate_mm, 3, j)
             run(add_bias, 3, j)
         run(weigh, *ks[3])
-        run(exp_z, 5)
+        run(exp_z, 2, 1)
         for i in (2, 3):
             run(quant_kw, *ks[i])
         for j in range(4):
@@ -480,7 +482,7 @@ def tile_rodimustemperedgatestatewrite_d2p_kernel(
                 run(gate_mm, 3, j + 2)
                 run(add_bias, 3, j + 2)
             if j % 2:
-                run(exp_z, 6 + j // 2)
+                run(exp_z, 3, j // 2)
         run(load_k, 3)
         for pair in range(2):
             run(decay_sum, 0, pair)
@@ -490,7 +492,7 @@ def tile_rodimustemperedgatestatewrite_d2p_kernel(
         outs = [(nt, eh) for nt in range(4) for eh in range(2)]
         vs = [(2, 0), (2, 1), (3, 0), (3, 1)]
         for i in range(4):
-            run(softplus_log, 4 + i)
+            run(softplus_log, 2 + i // 2, i % 2)
             if i in (1, 3):
                 run(turn_v_mm, *vs[i // 2])
                 run(empty_v, *vs[i // 2])
@@ -501,14 +503,14 @@ def tile_rodimustemperedgatestatewrite_d2p_kernel(
             run(store, 0, i)
             if i % 2:
                 run(load_s0, 1, i // 2)
-            if i > 0:
-                run(softplus_large, 3 + i)
-        run(softplus_large, 7)
+            if i == 2:
+                run(softplus_large, 2)
+        run(softplus_large, 3)
         for h in range(2):
             run(quant_v, 2, h)
         for i in range(6):
-            if i < 4:
-                run(gate_log, 4 + i)
+            if i in (0, 2):
+                run(gate_log, 2 + i // 2)
             if i == 1:
                 run(turn_v_mm, 3, 0)
                 run(empty_v, 3, 0)
@@ -516,12 +518,12 @@ def tile_rodimustemperedgatestatewrite_d2p_kernel(
                 run(decay_mm, 1, i - 2)
             if i == 2:
                 run(turn_v, 3, 1, "S")
-            if 1 <= i < 5:
-                run(log_small, 3 + i)
+            if i in (1, 3):
+                run(log_small, 2 + i // 2)
             if i in (3, 4):
                 run(quant_v, 3, i - 3)
-            if i >= 2:
-                run(exponent, 2 + i)
+            if i in (3, 5):
+                run(exponent, i // 2 + 1)
         for pair in range(2):
             run(decay_sum, 1, pair)
         ks = [(2, 0), (3, 0), (2, 1), (3, 1)]
@@ -541,6 +543,6 @@ def tile_rodimustemperedgatestatewrite_d2p_kernel(
                 nt, eh = outs[i - 1]
                 run(finish, 1, nt, eh)
                 if nt == 3:
-                    run(store, 1, nt, slice(512 * eh, 512 * eh + 512))
+                    run(store, 1, nt, eh)
                 elif eh:
                     run(store, 1, nt)

from contextlib import ExitStack

import concourse.mybir as mybir
from concourse.masks import make_identity

F32 = mybir.dt.float32
BF16 = mybir.dt.bfloat16
I32 = mybir.dt.int32
U32 = mybir.dt.uint32
U8 = mybir.dt.uint8
FP8 = mybir.dt.float8_e4m3fn
FP8X4 = mybir.dt.float8_e4m3fn_x4
ACT = mybir.ActivationFunctionType
ALU = mybir.AluOpType

B, T, D, N, E = 2, 1024, 1024, 512, 1024
P = 128
J = 4
CH = 512
FLOPS = 2 * (2 * B * T * D * N) + 2 * B * T * N * E

EXACT_ABOVE = 20.0
LOG_BELOW = -8.0


def tile_rodimustemperedgatestatewrite_d2p_kernel(
    tc, x_bytes, x_scale, wg_words, wg_scales, bg, wt_words, wt_scales, k, v, s0, out
):
    nc = tc.nc
    with ExitStack() as ctx:
        pool = ctx.enter_context(tc.tile_pool(name="sb", bufs=1))
        psum = ctx.enter_context(tc.psum_pool(name="ps", bufs=1))
        ctx.enter_context(tc.manual_schedule())

        chunks = [(b, g) for b in range(B) for g in range(2)]
        xb, vraw, kt, wr = {}, {}, {}, {}

        def buffers(name, count, shape, dtype):
            return [pool.tile(shape, dtype, name="%s%d" % (name, i), align_bytes=64) for i in range(count)]

        def banks(name, count):
            return [psum.tile([P, 512], F32, name="%s%d" % (name, i)) for i in range(count)]

        xb_buf = buffers("xb", 2, [P, J, D], U8)
        xw_buf = buffers("xw", 4, [P, 2, D], BF16)
        xg_buf = buffers("xg", 3, [P, 4 * CH], BF16)
        xq_buf = buffers("xq", 2, [P, 2, CH], U32)
        xqs_buf = buffers("xqs", 2, [P, 2, CH], U8)
        zb_buf = buffers("zb", 3, [P, J, N], F32)
        gt_buf = buffers("gt", 3, [P, J, N], F32)
        th_buf = buffers("th", 3, [P, J, 4, 130], F32)
        lg_buf = buffers("lg", 2, [P, J, N], F32)
        ot_buf = [lg_buf[1][:, 2 * i : 2 * i + 2, :].rearrange("p j n -> p (j n)") for i in range(2)]
        kt_buf = buffers("kt", 3, [P, J, N], BF16)
        kwg_buf = buffers("kwg", 3, [P, 256, J], BF16)
        kwq_buf = buffers("kwq", 4, [P, N], U32)
        kwqs_buf = buffers("kwqs", 4, [P, N], U8)
        vraw_buf = buffers("vraw", 4, [P, J, 512], BF16)
        vg_buf = buffers("vg", 2, [P, 512, J], BF16)
        vq_buf = buffers("vq", 4, [P, E], U32)
        vqs_buf = buffers("vqs", 4, [P, E], U8)
        s0_buf = buffers("s0t", 2, [P, 2, E], BF16)
        acc = buffers("acc", 2, [P, 4], F32)
        dec = buffers("dec", 2, [P, 4], F32)
        md_buf = buffers("md", 2, [P, 130], F32)
        xt_bank = banks("xt", 2)
        zg_bank = banks("zg", 2)
        zt_bank = banks("zt", 2)
        wr_bank = banks("wr", 2)
        for t in th_buf:
            nc.gpsimd.memset(t[:, :, :, 128:130], 1.0)

        def load_x(c, parts=1):
            b, g = chunks[c]
            xb[c] = xb_buf[c % 2]
            src = x_bytes[b, CH * g : CH * (g + 1), :].rearrange("(p j) d -> p j d", j=J)
            r = J // parts
            for h in range(parts):
                nc.sync.dma_start(out=xb[c][:, r * h : r * h + r, :], in_=src[:, r * h : r * h + r, :])

        def load_k(c):
            b, g = chunks[c]
            kt[c] = kt_buf[c % 3]
            nc.sync.dma_start(out=kt[c][:], in_=k[b, CH * g : CH * (g + 1), :].rearrange("(p j) n -> p j n", j=J))

        def load_v(c, h):
            b, g = chunks[c]
            vraw[c, h] = vraw_buf[(2 * c + h) % 4]
            src = v[b, CH * g : CH * (g + 1), 512 * h : 512 * h + 512].rearrange("(p j) e -> p j e", j=J)
            nc.sync.dma_start(out=vraw[c, h][:], in_=src)

        load_x(0, 2)
        xs = pool.tile([P, B, 2, 8], F32, name="xs")
        xs_src = x_scale.rearrange("b (g q) i -> q b g i", q=4)
        for q in range(4):
            nc.scalar.dma_start(out=xs[32 * q : 32 * q + 32, :, :, :], in_=xs_src[q].partition_broadcast(32))
        ident = pool.tile([P, P], F32, name="ident")
        make_identity(nc, ident[:])
        ws = pool.tile([P, 4, N], U8, name="ws", align_bytes=64)
        nc.gpsimd.memset(ws[:].rearrange("p i n -> p (i n)").bitcast(I32), 0)
        warm = pool.tile([P, 1], F32, name="warm")
        nc.vector.memset(warm[:], 0.0)
        nc.scalar.activation(out=warm[:], in_=warm[:], func=ACT.Tanh)
        brow = pool.tile([P, N], BF16, name="brow")
        nc.vector.memset(brow[:], 0.0)
        ones = pool.tile([P, P], BF16, name="ones")
        nc.vector.memset(ones[:], 1.0)
        eye = pool.tile([P, P], BF16, name="eye")
        nc.vector.tensor_copy(out=eye[:], in_=ident[:])
        nc.scalar.dma_start(out=brow[0:1, :], in_=bg.rearrange("(o n) -> o n", o=1))
        wq = [pool.tile([P, 2, N], I32, name="wq%d" % w, align_bytes=64) for w in range(2)]
        load_x(1, 2)
        for w, words in enumerate((wg_words, wt_words)):
            nc.sync.dma_start(out=wq[w][:], in_=words.rearrange("g p n t -> p g (n t)").bitcast(I32))
        for w, scl in enumerate((wg_scales, wt_scales)):
            for q in range(4):
                nc.sync.dma_start(
                    out=ws[32 * q : 32 * q + 4, 2 * w : 2 * w + 2, :].bitcast(I32),
                    in_=scl[:, 4 * q : 4 * q + 4, :].rearrange("g r n -> r g n").bitcast(I32),
                )
        mask = pool.tile([P, 130], F32, name="mask")
        nc.vector.memset(mask[:, 128:130], 0.5)
        nc.vector.tensor_copy(out=mask[:, 0:128], in_=ident[:])
        bias = pool.tile([P, N], F32, name="bias")

        def load_bias():
            wr["bias"] = wr_bank[0]
            nc.tensor.matmul(wr["bias"][:], lhsT=ones[:], rhs=brow[:], start=True, stop=True)

        def keep_bias():
            nc.scalar.copy(out=bias[:], in_=wr["bias"][:])

        xw, xt, xg, xq, xqs = {}, {}, {}, {}, {}

        def widen(c, s, jj, eng):
            b, g = chunks[c]
            h, gp = divmod(s, 2)
            xw[c, h] = xw_buf[(2 * c + h) % 4]
            for i in range(4 * gp, 4 * gp + 4):
                o = xw[c, h][:, jj, 128 * i : 128 * i + 128]
                a = xb[c][:, 2 * h + jj, 128 * i : 128 * i + 128].bitcast(FP8)
                sc = xs[:, b, g, i : i + 1]
                if eng == "A":
                    nc.any.tensor_scalar(out=o, in0=a, scalar1=sc, scalar2=None, op0=ALU.mult)
                elif eng == "S":
                    nc.scalar.activation(out=o, in_=a, func=ACT.Copy, scale=sc)
                else:
                    nc.vector.tensor_scalar(out=o, in0=a, scalar1=sc, scalar2=None, op0=ALU.mult)

        def copy(eng, out, in_):
            if eng == "A":
                nc.any.tensor_copy(out=out, in_=in_)
            elif eng == "S":
                nc.scalar.copy(out=out, in_=in_)
            else:
                nc.vector.tensor_copy(out=out, in_=in_)

        def turn_x(c, s):
            h, gp = divmod(s, 2)
            xt[c, s] = xt_bank[s % 2][:].rearrange("p (u r) -> p u r", u=2)
            for jj in range(2):
                wv = xw[c, h][:, jj, :].bitcast(F32)
                for u in range(2):
                    nc.tensor.transpose(
                        xt[c, s][:, u, 128 * jj : 128 * jj + 128], wv[:, 256 * gp + u : 256 * gp + 256 : 2], ident[:]
                    )

        def empty_x(c, s, eng):
            h, gp = divmod(s, 2)
            xg[c, gp] = xg_buf[(2 * c + gp) % 3]
            copy(
                eng,
                out=xg[c, gp][:, 1024 * h : 1024 * h + 1024].bitcast(F32).rearrange("p (r u) -> p r u", u=2),
                in_=xt[c, s].rearrange("p u r -> p r u"),
            )

        def quant_x(c, gp):
            xq[c], xqs[c] = xq_buf[c % 2], xqs_buf[c % 2]
            nc.vector.quantize_mx(out=xq[c][:, gp, :].bitcast(FP8X4), scales=xqs[c][:, gp, :], in_=xg[c, gp][:])

        zb, gt, zz, th = {}, {}, {}, {}

        def part(h):
            return slice(2 * h[0], 2 * h[0] + 2) if h else slice(0, J)

        def gate_mm(c, j):
            for w in range(2):
                z = (zg_bank, zt_bank)[w][j % 2]
                zz[c, j, w] = z
                for gp in range(2):
                    nc.tensor.matmul_mx(
                        out=z[:],
                        lhsT=xq[c][:, gp, 128 * j : 128 * j + 128].bitcast(FP8X4),
                        lhsT_scale=xqs[c][:, gp, 128 * j : 128 * j + 128],
                        rhs=wq[w][:, gp, :].bitcast(FP8X4),
                        rhs_scale=ws[:, 2 * w + gp, :],
                        start=(gp == 0),
                        stop=(gp == 1),
                    )

        def add_bias(c, j):
            zb[c] = zb_buf[c % 3]
            nc.vector.tensor_tensor(out=zb[c][:, j, :], in0=zz[c, j, 0][:], in1=bias[:], op=ALU.add)

        def tau(c, j):
            th[c] = th_buf[c % 3]
            nc.scalar.activation(
                out=th[c][:, j, :, 0:128], in_=zz[c, j, 1][:].rearrange("p (t n) -> p t n", t=4), func=ACT.Tanh, scale=0.5
            )

        def exp_z(c, *h):
            gt[c] = gt_buf[c % 3]
            s = part(h)
            nc.scalar.activation(out=gt[c][:, s, :], in_=zb[c][:, s, :], func=ACT.Exp)

        vg, vq, vqs = {}, {}, {}

        def turn_v(c, h, eng):
            vg[c, h] = vg_buf[h]
            copy(
                eng,
                out=vg[c, h][:].rearrange("p (c i) j -> p c j i", i=4),
                in_=vraw[c, h][:].rearrange("p j (c i) -> p c j i", i=4),
            )

        def turn_v_mm(c, h):
            for i in range(4):
                nc.tensor.matmul(
                    xt_bank[i // 2][:].bitcast(BF16)[:, 512 * (i % 2) : 512 * (i % 2) + 512].rearrange("p (e j) -> p e j", j=J),
                    lhsT=eye[:],
                    rhs=vraw[c, h][:, :, 128 * i : 128 * i + 128].rearrange("p j e -> p e j"),
                    start=True,
                    stop=True,
                )

        def empty_v(c, h, eng="S"):
            vg[c, h] = vg_buf[h]
            flat = vg[c, h][:].rearrange("p e j -> p (e j)")
            for i in range(2):
                copy(eng, out=flat[:, 1024 * i : 1024 * i + 1024], in_=xt_bank[i][:].bitcast(BF16))

        def quant_v(c, h):
            vq[c], vqs[c] = vq_buf[c], vqs_buf[c]
            e = slice(512 * h, 512 * h + 512)
            nc.vector.quantize_mx(
                out=vq[c][:, e].bitcast(FP8X4), scales=vqs[c][:, e], in_=vg[c, h][:].rearrange("p e j -> p (e j)")
            )

        def softplus_log(c, *h):
            s = part(h)
            nc.scalar.activation(out=gt[c][:, s, :], in_=gt[c][:, s, :], func=ACT.Ln, bias=1.0)

        def softplus_large(c, *h):
            s = part(h)
            nc.vector.scalar_tensor_tensor(
                out=gt[c][:, s, :], in0=gt[c][:, s, :], scalar=EXACT_ABOVE, in1=zb[c][:, s, :], op0=ALU.min, op1=ALU.max
            )

        lg = {}

        def gate_log(c, *h):
            s = part(h)
            nc.scalar.activation(out=lg_buf[c % 2][:, s, :], in_=gt[c][:, s, :], func=ACT.Ln)

        def log_small(c, *h):
            s = part(h)
            nc.vector.scalar_tensor_tensor(
                out=zb[c][:, s, :], in0=lg_buf[c % 2][:, s, :], scalar=LOG_BELOW, in1=zb[c][:, s, :], op0=ALU.max, op1=ALU.min
            )

        def exponent(c, *h):
            s = part(h)
            zv = zb[c][:, s, :].rearrange("p j (t n) -> p j t n", t=4)
            nc.vector.scalar_tensor_tensor(
                out=zv, in0=th[c][:, s, :, 0:128], scalar=1.0, in1=zv, op0=ALU.add, op1=ALU.mult
            )

        dg = {}

        def decay_mm(b, pair):
            dg[b, pair] = wr_bank[pair][:, 0:260].rearrange("p (q n) -> p q n", q=2)
            units = [(2 * b + g, j) for g in range(2) for j in range(J)]
            for q in range(2):
                nt = 2 * pair + q
                for n, (c, j) in enumerate(units):
                    nc.tensor.matmul(
                        dg[b, pair][:, q, :],
                        lhsT=gt[c][:, j, 128 * nt : 128 * nt + 128],
                        rhs=th[c][:, j, nt, :],
                        start=(n == 0),
                        stop=(n == len(units) - 1),
                    )

        def decay_sum(b, pair):
            for q in range(2):
                nt = 2 * pair + q
                nc.vector.scalar_tensor_tensor(
                    out=md_buf[q][:],
                    in0=dg[b, pair][:, q, :],
                    scalar=1.0,
                    in1=mask[:],
                    op0=ALU.mult,
                    op1=ALU.mult,
                    accum_out=acc[b][:, nt : nt + 1],
                )

        def decay_exp(b):
            nc.scalar.activation(out=dec[b][:], in_=acc[b][:], func=ACT.Exp, scale=-0.5 / T)

        kwq, kwqs, kwg = {}, {}, {}

        def tempered(c, *h):
            n = slice(256 * h[0], 256 * h[0] + 256) if h else slice(0, N)
            nc.scalar.activation(out=zb[c][:, :, n], in_=zb[c][:, :, n], func=ACT.Exp, scale=0.5)

        def weigh(c, h):
            n = slice(256 * h, 256 * h + 256)
            kwg[c, h] = kwg_buf[(2 * c + h) % 3]
            nc.vector.tensor_tensor(
                out=kwg[c, h][:].rearrange("p (c i) j -> p c j i", i=4),
                in0=zb[c][:, :, n].rearrange("p j (c i) -> p c j i", i=4),
                in1=kt[c][:, :, n].rearrange("p j (c i) -> p c j i", i=4),
                op=ALU.mult,
            )

        def quant_kw(c, h):
            n = slice(256 * h, 256 * h + 256)
            kwq[c], kwqs[c] = kwq_buf[c], kwqs_buf[c]
            nc.vector.quantize_mx(
                out=kwq[c][:, n].bitcast(FP8X4), scales=kwqs[c][:, n], in_=kwg[c, h][:].rearrange("p n j -> p (n j)")
            )

        s0t, ot = {}, {}

        def load_s0(b, pair):
            s0t[b, pair] = s0_buf[pair]
            nc.sync.dma_start(
                out=s0t[b, pair][:], in_=s0[b, 256 * pair : 256 * pair + 256, :].rearrange("(q p) e -> p q e", p=P)
            )

        def write_mm(b, nt, eh):
            wr[b, nt, eh] = (zg_bank, zt_bank)[nt % 2][eh]
            e = slice(512 * eh, 512 * eh + 512)
            n = slice(128 * nt, 128 * nt + 128)
            for g in range(2):
                c = 2 * b + g
                nc.tensor.matmul_mx(
                    out=wr[b, nt, eh][:],
                    lhsT=kwq[c][:, n].bitcast(FP8X4),
                    lhsT_scale=kwqs[c][:, n],
                    rhs=vq[c][:, e].bitcast(FP8X4),
                    rhs_scale=vqs[c][:, e],
                    start=(g == 0),
                    stop=(g == 1),
                )

        def finish(b, nt, eh):
            ot[b, nt] = ot_buf[nt % 2] if nt < 2 else xg_buf[nt % 2][:].bitcast(F32)
            e = slice(512 * eh, 512 * eh + 512)
            nc.vector.scalar_tensor_tensor(
                out=ot[b, nt][:, e],
                in0=s0t[b, nt // 2][:, nt % 2, e],
                scalar=dec[b][:, nt : nt + 1],
                in1=wr[b, nt, eh][:],
                op0=ALU.mult,
                op1=ALU.add,
            )

        def store(b, nt, *half):
            cols = slice(512 * half[0], 512 * half[0] + 512) if half else slice(0, E)
            nc.sync.dma_start(out=out[b, P * nt : P * nt + P, cols], in_=ot[b, nt][:, cols])

        def run(fn, *args):
            fn(*args)


        for s in range(5):
            if s < 4:
                run(widen, 0, s, 0, "V")
                run(widen, 0, s, 1, "S" if s < 2 else "V")
                run(turn_x, 0, s)
            if s > 0:
                run(empty_x, 0, s - 1, "S")
        run(load_bias)
        run(load_x, 2)
        run(load_v, 0, 0)
        run(load_v, 0, 1)
        for s in range(4):
            run(widen, 1, s, 0, "V")
            run(widen, 1, s, 1, "V")
            run(turn_x, 1, s)
            if s == 0:
                run(keep_bias)
            if s < 2:
                run(quant_x, 0, s)
            run(empty_x, 1, s, "S")
        run(load_x, 3)
        run(load_v, 1, 0)
        run(load_v, 1, 1)
        for c in range(3):
            run(load_k, c)
        run(load_s0, 0, 0)
        run(load_s0, 0, 1)
        for c in range(2):
            for j in range(4):
                run(gate_mm, c, j)
                run(widen, c + 2, j, 0, "V")
                run(widen, c + 2, j, 1, "V")
                run(add_bias, c, j)
                run(tau, c, j)
                if j % 2:
                    run(exp_z, c, j // 2)
                if c == 0 and j < 2:
                    run(quant_x, 1, j)
                s = 4 * c + j - 2
                if 0 <= s < 4:
                    run(turn_x, 2, s)
                    run(empty_x, 2, s, "S")
        for i in range(5):
            if i < 4:
                run(softplus_log, i // 2, i % 2)
                run(turn_x, 3, i)
            if i > 0:
                run(empty_x, 3, i - 1, "S")
            if i < 2:
                run(turn_v, 0, i, "V")
                run(quant_x, 2, i)
            if i in (1, 2):
                run(gate_mm, 2, i - 1)
            if i > 0:
                run(softplus_large, (i - 1) // 2, (i - 1) % 2)
            if i in (2, 3):
                run(quant_v, 0, i - 2)
        run(load_v, 2, 0)
        run(load_v, 2, 1)
        run(turn_v_mm, 1, 0)
        run(decay_mm, 0, 0)
        for i in range(6):
            if i < 4:
                run(gate_log, i // 2, i % 2)
            if i == 1:
                run(empty_v, 1, 0)
            if i in (0, 1):
                run(add_bias, 2, i)
                run(quant_x, 3, i)
            if 1 <= i < 5:
                run(log_small, (i - 1) // 2, (i - 1) % 2)
            if i in (3, 5):
                run(exponent, i // 2 - 1)
        run(turn_v_mm, 1, 1)
        run(empty_v, 1, 1)
        ks = [(0, 0), (0, 1), (1, 0), (1, 1)]
        for i in range(4):
            run(tau, 2, i)
            if i < 2:
                run(gate_mm, 2, i + 2)
                run(add_bias, 2, i + 2)
            if i == 1:
                run(decay_mm, 0, 1)
            if i == 1:
                run(tempered, 0)
            if i == 3:
                run(tempered, 1)
            if i >= 1:
                run(weigh, *ks[i - 1])
            if i < 2:
                run(quant_v, 1, i)
            if i >= 2:
                run(quant_kw, *ks[i - 2])
        run(exp_z, 2, 0)

        for j in range(2):
            run(gate_mm, 3, j)
            run(add_bias, 3, j)
        run(weigh, *ks[3])
        run(exp_z, 2, 1)
        for i in (2, 3):
            run(quant_kw, *ks[i])
        for j in range(4):
            run(tau, 3, j)
            if j < 2:
                run(gate_mm, 3, j + 2)
                run(add_bias, 3, j + 2)
            if j % 2:
                run(exp_z, 3, j // 2)
        run(load_k, 3)
        for pair in range(2):
            run(decay_sum, 0, pair)
        run(decay_exp, 0)
        run(load_v, 3, 0)
        run(load_v, 3, 1)
        outs = [(nt, eh) for nt in range(4) for eh in range(2)]
        vs = [(2, 0), (2, 1), (3, 0), (3, 1)]
        for i in range(4):
            run(softplus_log, 2 + i // 2, i % 2)
            if i in (1, 3):
                run(turn_v_mm, *vs[i // 2])
                run(empty_v, *vs[i // 2])
            for q in range(2):
                run(write_mm, 0, *outs[2 * i + q])
            for q in range(2):
                run(finish, 0, *outs[2 * i + q])
            run(store, 0, i)
            if i % 2:
                run(load_s0, 1, i // 2)
            if i == 2:
                run(softplus_large, 2)
        run(softplus_large, 3)
        for h in range(2):
            run(quant_v, 2, h)
        for i in range(6):
            if i in (0, 2):
                run(gate_log, 2 + i // 2)
            if i == 1:
                run(turn_v_mm, 3, 0)
                run(empty_v, 3, 0)
            if i in (2, 3):
                run(decay_mm, 1, i - 2)
            if i == 2:
                run(turn_v, 3, 1, "S")
            if i in (1, 3):
                run(log_small, 2 + i // 2)
            if i in (3, 4):
                run(quant_v, 3, i - 3)
            if i in (3, 5):
                run(exponent, i // 2 + 1)
        for pair in range(2):
            run(decay_sum, 1, pair)
        ks = [(2, 0), (3, 0), (2, 1), (3, 1)]
        for i in range(6):
            if i < 4:
                run(tempered, *ks[i])
            if i == 3:
                run(decay_exp, 1)
            if 1 <= i < 5:
                run(weigh, *ks[i - 1])
            if i >= 2:
                run(quant_kw, *ks[i - 2])
        for i in range(9):
            if i < 8:
                run(write_mm, 1, *outs[i])
            if i > 0:
                nt, eh = outs[i - 1]
                run(finish, 1, nt, eh)
                if nt == 3:
                    run(store, 1, nt, eh)
                elif eh:
                    run(store, 1, nt)
